import numpy as np
import ml_dtypes


def mxq(x, axis, fmt="e4m3"):
    dtype, down = {"e4m3": (ml_dtypes.float8_e4m3fn, 7), "e5m2": (ml_dtypes.float8_e5m2, 14)}[fmt]
    v = np.moveaxis(np.asarray(x, np.float32).astype(ml_dtypes.bfloat16).astype(np.float64), axis, -1)
    blocks = v.reshape(v.shape[:-1] + (-1, 32))
    amax = np.abs(blocks).max(-1, keepdims=True)
    byte = np.maximum(np.where(amax > 0, np.frexp(amax)[1] - 1 + 127, 0) - down, 1)
    scale = np.exp2(byte - 127.0)
    codes = (blocks / scale).astype(np.float32).astype(dtype).astype(np.float64)
    return np.moveaxis((codes * scale).reshape(v.shape), -1, axis)


WIDE = False


def mx_kscale(k):
    if not WIDE:
        return np.ones(k)
    levels = np.array([10, -10, 5, -5, 0])
    if k % 512:
        return np.exp2(np.random.permutation(np.resize(levels, k // 32))).repeat(32)
    a = np.empty((k // 512, 16))
    for p in range(k // 512):
        a[p, :8] = np.random.permutation(np.resize(levels, 8))
        for g in range(8):
            far = levels[np.abs(levels - a[p, g]) >= 10]
            a[p, g + 8] = far[np.random.randint(len(far))]
    return np.exp2(a.ravel()).repeat(32)


def f64(x):
    return np.asarray(x).astype(np.float64)


def striped(idx):
    return np.tile(idx.reshape(-1, 16).T, (8, 1)).astype(np.uint16)


def unstriped(offs):
    return offs[:16].T.reshape(-1).astype(np.int64)


E2M1 = np.array([0.0, 0.5, 1.0, 1.5, 2.0, 3.0, 4.0, 6.0, -0.0, -0.5, -1.0, -1.5, -2.0, -3.0, -4.0, -6.0])


def pack_weight(w, fmt):
    k, n = w.shape
    w = f64(np.asarray(w, np.float32).astype(ml_dtypes.bfloat16)).reshape(k // 32, 32, n)
    amax = np.abs(w).max(1)
    if fmt == "e4m3":
        byte = np.frexp(amax)[1] - 1 + 127 - 7
    else:
        mant, ex = np.frexp(amax / 6.0)
        byte = np.where(mant > 0.5, ex, ex - 1) + 127
    byte = np.clip(np.where(amax > 0, byte, 1), 1, 254)
    scaled = (w * np.exp2(127.0 - byte)[:, None, :]).reshape(k, n).astype(np.float32)
    by_word = np.ascontiguousarray(scaled.reshape(k // 512, 128, 4, n).transpose(0, 1, 3, 2))
    if fmt == "e4m3":
        words = by_word.astype(ml_dtypes.float8_e4m3fn).view(np.uint8)
    else:
        c = by_word.astype(ml_dtypes.float4_e2m1fn).view(np.uint8) & 0xF
        words = (c[..., 0::2] | (c[..., 1::2] << 4)).reshape(k // 512, 128, 2 * n)
    return np.ascontiguousarray(words), np.ascontiguousarray(byte.astype(np.uint8).reshape(k // 512, 16, n))


def unpack_weight(words, scales, fmt):
    g, _, n = scales.shape
    words = np.ascontiguousarray(words).reshape(g, 128, n, -1)
    if fmt == "e4m3":
        vals = words.view(ml_dtypes.float8_e4m3fn).astype(np.float64)
    else:
        nib = np.empty((g, 128, n, 4), np.uint8)
        nib[..., 0::2] = words & 0xF
        nib[..., 1::2] = words >> 4
        vals = E2M1[nib]
    vals = vals * np.repeat(np.exp2(scales.astype(np.float64) - 127.0), 8, axis=1)[..., None]
    return vals.transpose(0, 1, 3, 2).reshape(g * 512, n)


def gelu(v):
    return 0.5 * v * (1.0 + np.tanh(np.sqrt(2.0 / np.pi) * (v + 0.044715 * v**3)))


def bf(x):
    return np.asarray(x, np.float32).astype(ml_dtypes.bfloat16)


def planes(Y):
    n, m = Y.shape
    b = f64(bf(Y)).reshape(n // 32, 32, m)
    amax = np.abs(b).max(1)
    byte = np.clip(np.where(amax > 0, np.frexp(amax)[1] - 1 + 127 - 7, 1), 1, 254)
    codes = (b * np.exp2(127.0 - byte)[:, None, :]).reshape(n, m).astype(np.float32).astype(ml_dtypes.float8_e4m3fn).view(np.uint8)
    words = codes.reshape(n // 512, 128, 4, m).transpose(0, 1, 3, 2)
    return np.ascontiguousarray(words), np.ascontiguousarray(byte.astype(np.uint8).reshape(n // 512, 16, m))


K, K3, H, N, T, T2, S, P = 1024, 512, 1024, 512, 2048, 2048, 512, 1024

def setup_inputs():
    n = np.random.standard_normal
    s, s3, u = mx_kscale(K)[:, None], mx_kscale(K3)[:, None], mx_kscale(H)[:, None]
    amp = np.exp(0.8 * n(N))[None, :]
    perm = np.random.permutation(T2)
    d = {}
    d["tab_words"], d["tab_scales"] = pack_weight(n((K, T)) * s, "e4m3")
    d["offs"] = striped(np.random.permutation(T)[:S])
    d["tab2_words"], d["tab2_scales"] = pack_weight(n((K, T)) * s, "e4m3")
    d["offs2"] = striped(np.random.permutation(T)[:S])
    d["offs3"] = striped(perm[:S])
    d["offs4"] = striped(perm[S:2 * S])
    d["offs5"] = striped(np.random.permutation(T2)[:P])
    d["w1_words"], d["w1_scales"] = pack_weight(n((K, H)) / K**0.5 / s, "e2m1")
    d["wd"] = (n((K3, H)) / K3**0.5 / s3).astype(np.float32)
    d["dies"] = (n((K3, S)) * s3).astype(np.float32)
    d["g1"] = (1.3 * np.exp(0.3 * n(H)) * u[:, 0]).astype(np.float32)
    d["w3"] = (n((K, H)) / K**0.5 / s * u.T).astype(np.float32)
    d["air"] = (0.8 * n((H, S)) * u).astype(np.float32)
    d["wg1"] = np.exp(0.3 * n((128, S))).astype(np.float32)
    d["wg2"] = np.exp(0.3 * n((128, S))).astype(np.float32)
    d["page0"] = (n((H, T2)) * u).astype(np.float32)
    d["gain"] = np.exp(0.4 * n(H)).astype(np.float32)
    d["w5_words"], d["w5_scales"] = pack_weight(n((H, N)) / H**0.5 / u * amp, "e4m3")
    d["season"] = (0.8 * n((N, P)) * amp.T).astype(np.float32)
    return d

def reference(tab_words, tab_scales, offs, tab2_words, tab2_scales, offs2, offs3, offs4, offs5, w1_words, w1_scales, wd, dies, g1, w3, air, wg1, wg2, page0, gain, w5_words, w5_scales, season):
    v = unpack_weight(tab_words, tab_scales, "e4m3")[:, unstriped(offs)]
    v2 = unpack_weight(tab2_words, tab2_scales, "e4m3")[:, unstriped(offs2)]
    w1 = unpack_weight(w1_words, w1_scales, "e2m1")
    w5 = unpack_weight(w5_words, w5_scales, "e4m3")
    e1 = w1.T @ v + mxq(f64(wd), 0, "e4m3").T @ mxq(f64(dies), 0, "e4m3")
    h1 = f64(g1)[:, None] * np.tanh(e1)
    h2 = np.maximum(mxq(f64(w3), 0, "e4m3").T @ v2, f64(air))
    page = f64(page0).copy()
    page[:, unstriped(offs3)] = np.tile(f64(wg1), (H // 128, 1)) * h1
    page[:, unstriped(offs4)] = np.tile(f64(wg2), (H // 128, 1)) * h2
    x = f64(gain)[:, None] * page[:, unstriped(offs5)]
    y = (w5.T @ mxq(x, 0, "e4m3")) + f64(season)
    words, scales = planes(y)
    return y, words, scales

@@ -1,0 +1,325 @@
+from contextlib import ExitStack
+
+import concourse.mybir as mybir
+
+F32 = mybir.dt.float32
+BF16 = mybir.dt.bfloat16
+I32 = mybir.dt.int32
+U32 = mybir.dt.uint32
+U16 = mybir.dt.uint16
+U8 = mybir.dt.uint8
+FP8X4 = mybir.dt.float8_e4m3fn_x4
+FP4X4 = mybir.dt.float4_e2m1fn_x4
+ALU = mybir.AluOpType
+ACT = mybir.ActivationFunctionType
+
+P = 128
+K, K3, H, N, T, T2, S, PICK = 1024, 512, 1024, 512, 2048, 2048, 512, 1024
+FLOPS = 2 * (K * H * S + K3 * H * S + K * H * S + H * N * PICK)
+HALF = 512
+CH = 256
+
+
+def tile_list_pasta_crack_page_kernel(
+    tc, tab_words, tab_scales, offs, tab2_words, tab2_scales, offs2, offs3, offs4, offs5,
+    w1_words, w1_scales, wd, dies, g1, w3, air, wg1, wg2, page0, gain, w5_words, w5_scales, season,
+    out_0, out_1, out_2,
+):
+    nc = tc.nc
+    with ExitStack() as ctx:
+        lists = ctx.enter_context(tc.tile_pool(name="lists", bufs=1))
+        keep = ctx.enter_context(tc.tile_pool(name="keep", bufs=1))
+        ring = ctx.enter_context(tc.tile_pool(name="ring", bufs=3))
+        psum = ctx.enter_context(tc.psum_pool(name="psum", bufs=1))
+
+        def held(name, shape, dtype, tag=None):
+            return keep.tile(shape, dtype, name=name, tag=tag or name, align_bytes=64)
+
+        def load(dst, src):
+            nc.sync.dma_start(out=dst, in_=src)
+
+        def load_list(name, src):
+            tile = lists.tile(list(src.shape), U16, name=name)
+            nc.sync.dma_start(tile[:], src)
+            return tile
+
+        def load_rows4(name, slot, src):
+            tile = held(name, [P, 4, src.shape[1]], F32, tag=slot)
+            load(tile[:], src.rearrange("(p j) c -> p j c", j=4))
+            return tile
+
+        def load_words(name, slot, words, a):
+            tile = held(name, [P, T], I32, tag=slot)
+            load(tile[:], words[a].rearrange("p c i -> p (c i)").bitcast(I32))
+            return tile
+
+        def load_scales_side(queue, tile, scales):
+            for q in range(4):
+                queue.dma_start(out=tile[32 * q : 32 * q + 4, :, :].bitcast(I32),
+                                in_=scales.bitcast(I32)[:, 4 * q : 4 * q + 4, :].rearrange("a r c -> r a c"))
+
+        def load_scales_stacked(tile, scales):
+            for q in range(4):
+                load(tile[32 * q : 32 * q + 8, :].bitcast(I32), scales.bitcast(I32)[:, 4 * q : 4 * q + 4, :])
+
+        def load_wg(tile, wg, t0, t1):
+            rows = wg.rearrange("(m t) j -> m t j", t=4)
+            for q in range(4):
+                load(tile[32 * q : 32 * q + 32, :, :], rows[:, t0:t1, :])
+
+        def load_page(s):
+            b, t = divmod(s, 4)
+            tile = held("page%d" % s, [P, T2], F32)
+            load(tile[:], page0[HALF * b : HALF * (b + 1), :].rearrange("(p t) c -> p t c", t=4)[:, t, :])
+            return tile
+
+        tabs_raw = held("tabs_raw", [P, 2, T], U8)
+        w1s_raw = held("w1s_raw", [P, 2, H], U8)
+        tab2s_raw = held("tab2s_raw", [P, T], U8)
+        w5s_raw = held("w5s_raw", [P, N], U8)
+        nc.vector.memset(tabs_raw[:].bitcast(I32), 0)
+        nc.vector.memset(w1s_raw[:].bitcast(I32), 0)
+        nc.vector.memset(tab2s_raw[:].bitcast(I32), 0)
+        nc.vector.memset(w5s_raw[:].bitcast(I32), 0)
+        warm = held("warm", [P, 8], F32)
+        warm2 = held("warm2", [P, 8], F32)
+        nc.vector.memset(warm[:], 0.0)
+        nc.scalar.activation(warm2[:], warm[:], ACT.Tanh)
+
+        w1w_raw = held("w1w_raw", [P, 2, H // 2], I32, tag="wraw")
+        load(w1w_raw[:], w1_words.bitcast(I32).rearrange("a p c -> p a c"))
+        dies_raw = load_rows4("dies_raw", "dies_raw", dies)
+        l1 = load_list("l1", offs)
+        load_scales_side(nc.gpsimd, tabs_raw, tab_scales)
+        wd_raw = [load_rows4("wd_raw0", "wd_raw0", wd[:, 0:HALF])]
+        load_scales_side(nc.sync, w1s_raw, w1_scales)
+        tabw = [load_words("tabw0", "tabw0", tab_words, 0)]
+        g1_t = held("g1_t", [P, 2, 4], F32)
+        load(g1_t[:], g1.rearrange("(b p t) -> p b t", b=2, t=4))
+        l3 = load_list("l3", offs3)
+        tabw.append(load_words("tabw1", "tabw1", tab_words, 1))
+        wg1_rows = []
+        pages = []
+        for t0, t1 in ((0, 1), (1, 2), (2, 4)):
+            tile = held("wg1_%d" % t0, [P, t1 - t0, S], F32)
+            load_wg(tile, wg1, t0, t1)
+            wg1_rows.extend(tile[:, i, :] for i in range(t1 - t0))
+            pages.append(load_page(t0))
+        wd_raw.append(load_rows4("wd_raw1", "wd_raw1", wd[:, HALF:H]))
+        pages.append(load_page(3))
+
+        def cast_dealt(name, raw):
+            wide = ring.tile([P, 4 * HALF], BF16, name=name, tag="cast", bufs=2, align_bytes=64)
+            nc.scalar.copy(wide[:].rearrange("p (t m j) -> p m j t", t=4, j=4),
+                           raw[:].rearrange("p j (m t) -> p m j t", t=4))
+            return wide
+
+        def cast_plain(eng, dst, src):
+            out = dst.rearrange("p (c i j) -> p c j i", i=4, j=4)
+            in_ = src.rearrange("p j (c i) -> p c j i", i=4)
+            if eng == "scalar":
+                nc.scalar.copy(out, in_)
+            else:
+                nc.vector.tensor_copy(out, in_)
+
+        def quantise(name, tag, wide, cols, codes_tag=None):
+            codes = held(name + "_c", [P, cols], U32, tag=codes_tag or tag + "_c")
+            plane = held(name + "_s", [P, cols], U8, tag=tag + "_s")
+            nc.vector.quantize_mx(out=codes[:].bitcast(FP8X4), scales=plane[:], in_=wide)
+            return codes, plane
+
+        def bank(name, n):
+            return psum.tile([P, HALF], F32, name=name, tag="bank%d" % n)
+
+        w1w, w1s = [], []
+        for b in range(2):
+            ww = held("w1w%d" % b, [P, 2, 4, 2 * P], U8)
+            nc.vector.tensor_copy(
+                ww[:].rearrange("p a t (m e) -> p a t m e", e=2),
+                w1w_raw[:].bitcast(U8)[:, :, H * b : H * (b + 1)].rearrange("p a (m t e) -> p a t m e", t=4, e=2))
+            w1w.append(ww)
+        for b in range(2):
+            ws = held("w1s%d" % b, [P, 2, 4, P], U8)
+            nc.vector.tensor_copy(
+                ws[:], w1s_raw[:, :, HALF * b : HALF * (b + 1)].rearrange("p a (m t) -> p a t m", t=4))
+            w1s.append(ws)
+
+        dies_wide = ring.tile([P, 4 * S], BF16, name="dies_wide", tag="cast", bufs=2, align_bytes=64)
+        cast_plain("scalar", dies_wide[:], dies_raw[:])
+        wd_wide = cast_dealt("wd_wide0", wd_raw[0])
+        dies_q = quantise("dies", "dies", dies_wide[:], S)
+        vs = []
+        for a in range(2):
+            tile = held("vs%d" % a, [P, S], U8)
+            nc.vector.tensor_copy(tile[:], tabs_raw[:, a, :].indirect(l1[:]))
+            vs.append(tile)
+        wd_q = [quantise("wd0", "wd0", wd_wide[:], HALF, codes_tag="tabs_raw")]
+        vw = []
+        for a in range(2):
+            tile = held("vw%d" % a, [P, S], U32)
+            nc.vector.tensor_copy(tile[:], tabw[a][:].bitcast(U32).indirect(l1[:]))
+            vw.append(tile)
+
+        def h1_scatter(s):
+            b, t = divmod(s, 4)
+            cols = slice(P * t, P * (t + 1))
+            acc = bank("h1_%d" % s, 4 + t)
+            nc.tensor.matmul_mx(out=acc[:], lhsT=wd_q[b][0][:, cols].bitcast(FP8X4), lhsT_scale=wd_q[b][1][:, cols],
+                                rhs=dies_q[0][:].bitcast(FP8X4), rhs_scale=dies_q[1][:], start=True, stop=False)
+            for a in range(2):
+                nc.tensor.matmul_mx(out=acc[:], lhsT=w1w[b][:, a, t, :].bitcast(FP4X4), lhsT_scale=w1s[b][:, a, t, :],
+                                    rhs=vw[a][:].bitcast(FP8X4), rhs_scale=vs[a][:], start=False, stop=(a == 1))
+            th = ring.tile([P, S], F32, name="th%d" % s, tag="th")
+            nc.scalar.activation(th[:], acc[:], ACT.Tanh)
+            h1 = held("h1_sb%d" % s, [P, S], F32, tag=("wd_raw1", "w3_raw10")[b]) if t == 3 else th
+            nc.scalar.activation(h1[:], th[:], ACT.Copy, scale=g1_t[:, b, t : t + 1])
+            nc.vector.tensor_tensor(pages[s][:].indirect(l3[:]), h1[:], wg1_rows[t], ALU.mult)
+
+        for s in range(4):
+            if s == 3:
+                wd_q.append(quantise("wd1", "wd1", cast_dealt("wd_wide1", wd_raw[1])[:], HALF))
+            h1_scatter(s)
+
+        pages.append(load_page(4))
+        l2 = load_list("l2", offs2)
+        pages.append(load_page(5))
+        load_scales_stacked(tab2s_raw, tab2_scales)
+        tab2w = [load_words("tab2w0", "tab2w0", tab2_words, 0), load_words("tab2w1", "dies_raw", tab2_words, 1)]
+        pages.append(load_page(6))
+        w3_raw = {}
+        w3_raw[0, 0] = load_rows4("w3_raw00", "w3_raw00", w3[0:HALF, 0:HALF])
+        w3_raw[1, 0] = load_rows4("w3_raw10", "w3_raw10", w3[HALF:K, 0:HALF])
+        pages.append(load_page(7))
+        l4 = load_list("l4", offs4)
+        air_t = [load_rows4("air0", "air0", air[0:HALF, :])]
+        wg2_t = held("wg2_t", [P, 4, S], F32)
+        load_wg(wg2_t, wg2, 0, 4)
+        l5 = load_list("l5", offs5)
+        gain_t = held("gain_t", [P, 2, 4], F32)
+        load(gain_t[:], gain.rearrange("(b p t) -> p b t", b=2, t=4))
+
+        h1_scatter(4)
+        h1_scatter(5)
+        v2s = held("v2s", [P, S], U8)
+        nc.vector.tensor_copy(v2s[:], tab2s_raw[:].indirect(l2[:]))
+        v2w = []
+        for a in range(2):
+            tile = held("v2w%d" % a, [P, S], U32)
+            nc.vector.tensor_copy(tile[:], tab2w[a][:].bitcast(U32).indirect(l2[:]))
+            v2w.append(tile)
+        h1_scatter(6)
+        w3_q = {}
+        for a in range(2):
+            wide = cast_dealt("w3_wide%d0" % a, w3_raw[a, 0])
+            w3_q[a, 0] = quantise("w3_%d0" % a, "w3_%d" % a, wide[:], HALF)
+        h1_scatter(7)
+
+        w3_raw[0, 1] = load_rows4("w3_raw01", "wd_raw0", w3[0:HALF, HALF:H])
+        w3_raw[1, 1] = load_rows4("w3_raw11", "tabw0", w3[HALF:K, HALF:H])
+        air_t.append(load_rows4("air1", "tabw1", air[HALF:H, :]))
+        w5w_raw = held("w5w_raw", [P, 2, N], I32, tag="wraw")
+        load(w5w_raw[:], w5_words.rearrange("a p c i -> p a (c i)").bitcast(I32))
+        load_scales_stacked(w5s_raw, w5_scales)
+        season_rows = season.rearrange("(p t) j -> p t j", t=4)
+        y = []
+        for h in range(2):
+            tile = held("y%d" % h, [P, 4, HALF], F32, tag=("wd_raw1", "tab2w0")[h])
+            load(tile[:], season_rows[:, :, HALF * h : HALF * (h + 1)])
+            y.append(tile)
+
+        h2 = {}
+
+        def h2_max(s):
+            b, t = divmod(s, 4)
+            cols = slice(P * t, P * (t + 1))
+            acc = bank("h2_%d" % s, t)
+            for a in range(2):
+                nc.tensor.matmul_mx(out=acc[:], lhsT=w3_q[a, b][0][:, cols].bitcast(FP8X4),
+                                    lhsT_scale=w3_q[a, b][1][:, cols], rhs=v2w[a][:].bitcast(FP8X4),
+                                    rhs_scale=v2s[4 * a : P, :], start=(a == 0), stop=(a == 1))
+            h2[s] = ring.tile([P, S], F32, name="h2_sb%d" % s, tag="th")
+            nc.vector.tensor_tensor(h2[s][:], acc[:], air_t[b][:, t, :], ALU.max)
+
+        def h2_scatter(s):
+            nc.vector.tensor_tensor(pages[s][:].indirect(l4[:]), h2[s][:], wg2_t[:, s % 4, :], ALU.mult)
+
+        small_tags = ("vw0", "vw1", "w1w0", "w1w1")
+        x0_wide = held("x0_wide", [P, PICK, 4], BF16, tag="w3_raw00")
+        x1_wide = [held("x1_wide%d" % c, [P, CH, 4], BF16, tag=small_tags[c]) for c in range(PICK // CH)]
+
+        def gained(s, dst, src):
+            b, t = divmod(s, 4)
+            nc.scalar.activation(dst[:, :, t], src, ACT.Copy, scale=gain_t[:, b, t : t + 1])
+
+        def pick(s):
+            picked = ring.tile([P, PICK], F32, name="picked%d" % s, tag="picked", bufs=2)
+            nc.vector.tensor_copy(picked[:], pages[s][:].indirect(l5[:]))
+            if s < 4:
+                gained(s, x0_wide, picked[:])
+            else:
+                for c in range(PICK // CH):
+                    gained(s, x1_wide[c], picked[:, CH * c : CH * (c + 1)])
+
+        h2_max(0)
+        h2_max(1)
+        h2_scatter(0)
+        for s in range(1, 8):
+            if s < 7:
+                h2_max(s + 1)
+            if s == 2:
+                for a in range(2):
+                    wide = cast_dealt("w3_wide%d1" % a, w3_raw[a, 1])
+                    w3_q[a, 1] = quantise("w3_%d1" % a, "w3_%d" % a, wide[:], HALF)
+            if s < 7:
+                h2_scatter(s)
+            pick(s - 1)
+            if s == 4:
+                w5w = held("w5w", [P, 2, 4, P], I32)
+                nc.vector.tensor_copy(w5w[:], w5w_raw[:].rearrange("p a (m t) -> p a t m", t=4))
+                w5s = held("w5s", [P, 4, P], U8)
+                nc.vector.tensor_copy(w5s[:], w5s_raw[:].rearrange("p (m t) -> p t m", t=4))
+            if s == 5:
+                x0_q = quantise("x0", "x0", x0_wide[:].rearrange("p c t -> p (c t)"), PICK, codes_tag="tabs_raw")
+        h2_scatter(7)
+
+        def y_pass(acc, a, t, codes, plane, start, stop):
+            nc.tensor.matmul_mx(out=acc, lhsT=w5w[:, a, t, :].bitcast(FP8X4), lhsT_scale=w5s[4 * a : P, t, :],
+                                rhs=codes.bitcast(FP8X4), rhs_scale=plane, start=start, stop=stop)
+
+        y_acc = {}
+        for h in range(2):
+            for t in range(4):
+                y_acc[h, t] = bank("y_%d%d" % (h, t), 4 * (1 - h) + t)
+                cols = slice(HALF * h, HALF * (h + 1))
+                y_pass(y_acc[h, t][:], 0, t, x0_q[0][:, cols], x0_q[1][:, cols], True, False)
+
+        last = ring.tile([P, PICK], F32, name="picked7", tag="picked", bufs=2)
+        for c in range(PICK // CH):
+            part = last[:, CH * c : CH * (c + 1)]
+            nc.vector.tensor_copy(part, pages[7][:].indirect(l5[:, CH // 16 * c : CH // 16 * (c + 1)]))
+            gained(7, x1_wide[c], part)
+
+        for c in range(PICK // CH):
+            h, u = divmod(c, 2)
+            codes, plane = quantise("x1_%d" % c, "x1_%d" % c, x1_wide[c][:].rearrange("p c t -> p (c t)"), CH)
+            for t in range(4):
+                y_pass(y_acc[h, t][:, CH * u : CH * (u + 1)], 1, t, codes[:], plane[:], False, u == 1)
+
+        out_rows = out_0.rearrange("(p t) j -> p t j", t=4)
+        out_words = out_1[0].rearrange("p m t -> p (m t)").bitcast(I32)
+        out_scales = out_2[0].bitcast(I32)
+        y_plane = held("y_plane", [P, PICK], U8)
+        y_codes = [held("y_codes%d" % c, [P, CH], I32) for c in range(PICK // CH)]
+        for h in range(2):
+            for t in range(4):
+                nc.vector.tensor_tensor(y[h][:, t, :], y_acc[h, t][:], y[h][:, t, :], ALU.add)
+                nc.sync.dma_start(out=out_rows[:, t, HALF * h : HALF * (h + 1)], in_=y[h][:, t, :])
+        for c in range(PICK // CH):
+            h, u = divmod(c, 2)
+            y_wide = held("y_wide%d" % c, [P, 4 * CH], BF16, tag=small_tags[c])
+            cast_plain("vector" if c == 3 else "scalar", y_wide[:], y[h][:, :, CH * u : CH * (u + 1)])
+            nc.vector.quantize_mx(out=y_codes[c][:].bitcast(FP8X4), scales=y_plane[:, CH * c : CH * (c + 1)],
+                                  in_=y_wide[:])
+            nc.sync.dma_start(out=out_words[:, CH * c : CH * (c + 1)], in_=y_codes[c][:])
+        for q in range(4):
+            nc.sync.dma_start(out=out_scales[4 * q : 4 * q + 4, :], in_=y_plane[32 * q : 32 * q + 4, :].bitcast(I32))

@@ -1,6 +1,7 @@
 from contextlib import ExitStack
 
 import concourse.mybir as mybir
+from concourse.masks import make_identity
 
 F32 = mybir.dt.float32
 BF16 = mybir.dt.bfloat16
@@ -62,11 +63,6 @@ def tile_list_pasta_crack_page_kernel(
             for q in range(4):
                 load(tile[32 * q : 32 * q + 8, :].bitcast(I32), scales.bitcast(I32)[:, 4 * q : 4 * q + 4, :])
 
-        def load_wg(tile, wg, t0, t1):
-            rows = wg.rearrange("(m t) j -> m t j", t=4)
-            for q in range(4):
-                load(tile[32 * q : 32 * q + 32, :, :], rows[:, t0:t1, :])
-
         def load_page(s):
             b, t = divmod(s, 4)
             tile = held("page%d" % s, [P, T2], F32)
@@ -77,8 +73,10 @@ def tile_list_pasta_crack_page_kernel(
         w1s_raw = held("w1s_raw", [P, 2, H], U8)
         tab2s_raw = held("tab2s_raw", [P, T], U8)
         w5s_raw = held("w5s_raw", [P, N], U8)
-        nc.vector.memset(tabs_raw[:].bitcast(I32), 0)
         nc.vector.memset(w1s_raw[:].bitcast(I32), 0)
+        nc.vector.memset(tabs_raw[:].bitcast(I32), 0)
+        ident = held("ident", [P, P], F32)
+        make_identity(nc, ident[:])
         nc.vector.memset(tab2s_raw[:].bitcast(I32), 0)
         nc.vector.memset(w5s_raw[:].bitcast(I32), 0)
         warm = held("warm", [P, 8], F32)
@@ -86,30 +84,31 @@ def tile_list_pasta_crack_page_kernel(
         nc.vector.memset(warm[:], 0.0)
         nc.scalar.activation(warm2[:], warm[:], ACT.Tanh)
 
+        wg1_raw = held("wg1_raw", [P, S], F32)
+        load(wg1_raw[:], wg1)
         w1w_raw = held("w1w_raw", [P, 2, H // 2], I32, tag="wraw")
         load(w1w_raw[:], w1_words.bitcast(I32).rearrange("a p c -> p a c"))
-        dies_raw = load_rows4("dies_raw", "dies_raw", dies)
         l1 = load_list("l1", offs)
-        load_scales_side(nc.gpsimd, tabs_raw, tab_scales)
-        wd_raw = [load_rows4("wd_raw0", "wd_raw0", wd[:, 0:HALF])]
-        load_scales_side(nc.sync, w1s_raw, w1_scales)
-        tabw = [load_words("tabw0", "tabw0", tab_words, 0)]
         g1_t = held("g1_t", [P, 2, 4], F32)
         load(g1_t[:], g1.rearrange("(b p t) -> p b t", b=2, t=4))
         l3 = load_list("l3", offs3)
+        dies_raw = load_rows4("dies_raw", "dies_raw", dies)
+        wd_raw = [load_rows4("wd_raw0", "wd_raw0", wd[:, 0:HALF])]
+        l2 = load_list("l2", offs2)
+        load_scales_side(nc.sync, tabs_raw, tab_scales)
+        tabw = [load_words("tabw0", "tabw0", tab_words, 0)]
+        load_scales_side(nc.sync, w1s_raw, w1_scales)
         tabw.append(load_words("tabw1", "tabw1", tab_words, 1))
-        wg1_rows = []
-        pages = []
-        for t0, t1 in ((0, 1), (1, 2), (2, 4)):
-            tile = held("wg1_%d" % t0, [P, t1 - t0, S], F32)
-            load_wg(tile, wg1, t0, t1)
-            wg1_rows.extend(tile[:, i, :] for i in range(t1 - t0))
-            pages.append(load_page(t0))
+        pages = [load_page(s) for s in range(2)]
+        wg2_raw = held("wg2_raw", [P, S], F32)
+        load(wg2_raw[:], wg2)
         wd_raw.append(load_rows4("wd_raw1", "wd_raw1", wd[:, HALF:H]))
+        load_scales_stacked(tab2s_raw, tab2_scales)
+        pages.append(load_page(2))
         pages.append(load_page(3))
 
-        def cast_dealt(name, raw):
-            wide = ring.tile([P, 4 * HALF], BF16, name=name, tag="cast", bufs=2, align_bytes=64)
+        def cast_dealt(name, raw, tag):
+            wide = held(name, [P, 4 * HALF], BF16, tag=tag)
             nc.scalar.copy(wide[:].rearrange("p (t m j) -> p m j t", t=4, j=4),
                            raw[:].rearrange("p j (m t) -> p m j t", t=4))
             return wide
@@ -131,6 +130,27 @@ def tile_list_pasta_crack_page_kernel(
         def bank(name, n):
             return psum.tile([P, HALF], F32, name=name, tag="bank%d" % n)
 
+        def spread_rows(name, raw, first_bank):
+            turned = bank(name + "_turned", first_bank)
+            for u in range(4):
+                nc.tensor.transpose(turned[:, P * u : P * (u + 1)], raw[:, P * u : P * (u + 1)], ident[:])
+            picked_cols = held(name + "_cols", [P, 4, 4, 4, 32], F32, tag="air0")
+            nc.scalar.copy(picked_cols[:],
+                           turned[:].rearrange("p (u m t) -> p u t m", u=4, t=4).unsqueeze(3).broadcast_to([P, 4, 4, 4, 32]))
+            return picked_cols
+
+        def spread_back(name, picked_cols):
+            rows = held(name + "_rows", [P, 4, S], F32)
+            for t in range(4):
+                back = bank(name + "_back%d" % t, t)
+                for u in range(4):
+                    nc.tensor.transpose(back[:, P * u : P * (u + 1)],
+                                        picked_cols[:, u, t, :, :].rearrange("p q m -> p (q m)"), ident[:])
+                nc.scalar.copy(rows[:, t, :], back[:])
+            return rows
+
+        wg1_cols = spread_rows("wg1", wg1_raw, 0)
+
         w1w, w1s = [], []
         for b in range(2):
             ww = held("w1w%d" % b, [P, 2, 4, 2 * P], U8)
@@ -138,15 +158,17 @@ def tile_list_pasta_crack_page_kernel(
                 ww[:].rearrange("p a t (m e) -> p a t m e", e=2),
                 w1w_raw[:].bitcast(U8)[:, :, H * b : H * (b + 1)].rearrange("p a (m t e) -> p a t m e", t=4, e=2))
             w1w.append(ww)
-        for b in range(2):
-            ws = held("w1s%d" % b, [P, 2, 4, P], U8)
+
+        def deal_w1_scales(b, tag):
+            ws = held("w1s%d" % b, [P, 2, 4, P], U8, tag=tag)
             nc.vector.tensor_copy(
                 ws[:], w1s_raw[:, :, HALF * b : HALF * (b + 1)].rearrange("p a (m t) -> p a t m", t=4))
             w1s.append(ws)
 
-        dies_wide = ring.tile([P, 4 * S], BF16, name="dies_wide", tag="cast", bufs=2, align_bytes=64)
-        cast_plain("scalar", dies_wide[:], dies_raw[:])
-        wd_wide = cast_dealt("wd_wide0", wd_raw[0])
+        dies_wide = held("dies_wide", [P, 4 * S], BF16, tag="cast0")
+        cast_plain("vector", dies_wide[:], dies_raw[:])
+        wd_wide = cast_dealt("wd_wide0", wd_raw[0], "cast1")
+        wg1_t = spread_back("wg1", wg1_cols)
         dies_q = quantise("dies", "dies", dies_wide[:], S)
         vs = []
         for a in range(2):
@@ -159,6 +181,7 @@ def tile_list_pasta_crack_page_kernel(
             tile = held("vw%d" % a, [P, S], U32)
             nc.vector.tensor_copy(tile[:], tabw[a][:].bitcast(U32).indirect(l1[:]))
             vw.append(tile)
+            deal_w1_scales(a, ("w1s0", "tabw1")[a])
 
         def h1_scatter(s):
             b, t = divmod(s, 4)
@@ -169,22 +192,24 @@ def tile_list_pasta_crack_page_kernel(
             for a in range(2):
                 nc.tensor.matmul_mx(out=acc[:], lhsT=w1w[b][:, a, t, :].bitcast(FP4X4), lhsT_scale=w1s[b][:, a, t, :],
                                     rhs=vw[a][:].bitcast(FP8X4), rhs_scale=vs[a][:], start=False, stop=(a == 1))
-            th = ring.tile([P, S], F32, name="th%d" % s, tag="th")
+            if s in (0, 2, 4, 5):
+                th = held("th%d" % s, [P, S], F32, tag="v2s" if s == 2 else "cast%d" % (s % 2))
+            else:
+                th = ring.tile([P, S], F32, name="th%d" % s, tag="th")
             nc.scalar.activation(th[:], acc[:], ACT.Tanh)
             h1 = held("h1_sb%d" % s, [P, S], F32, tag=("wd_raw1", "w3_raw10")[b]) if t == 3 else th
             nc.scalar.activation(h1[:], th[:], ACT.Copy, scale=g1_t[:, b, t : t + 1])
-            nc.vector.tensor_tensor(pages[s][:].indirect(l3[:]), h1[:], wg1_rows[t], ALU.mult)
+            nc.vector.tensor_tensor(pages[s][:].indirect(l3[:]), h1[:], wg1_t[:, t, :], ALU.mult)
 
         for s in range(4):
             if s == 3:
-                wd_q.append(quantise("wd1", "wd1", cast_dealt("wd_wide1", wd_raw[1])[:], HALF))
+                wd_q.append(quantise("wd1", "wd1", cast_dealt("wd_wide1", wd_raw[1], "cast0")[:], HALF))
             h1_scatter(s)
 
-        pages.append(load_page(4))
-        l2 = load_list("l2", offs2)
-        pages.append(load_page(5))
-        load_scales_stacked(tab2s_raw, tab2_scales)
+        wg2_t = spread_back("wg2", spread_rows("wg2", wg2_raw, 4))
         tab2w = [load_words("tab2w0", "tab2w0", tab2_words, 0), load_words("tab2w1", "dies_raw", tab2_words, 1)]
+        pages.append(load_page(4))
+        pages.append(load_page(5))
         pages.append(load_page(6))
         w3_raw = {}
         w3_raw[0, 0] = load_rows4("w3_raw00", "w3_raw00", w3[0:HALF, 0:HALF])
@@ -192,25 +217,20 @@ def tile_list_pasta_crack_page_kernel(
         pages.append(load_page(7))
         l4 = load_list("l4", offs4)
         air_t = [load_rows4("air0", "air0", air[0:HALF, :])]
-        wg2_t = held("wg2_t", [P, 4, S], F32)
-        load_wg(wg2_t, wg2, 0, 4)
         l5 = load_list("l5", offs5)
         gain_t = held("gain_t", [P, 2, 4], F32)
         load(gain_t[:], gain.rearrange("(b p t) -> p b t", b=2, t=4))
 
-        h1_scatter(4)
-        h1_scatter(5)
         v2s = held("v2s", [P, S], U8)
         nc.vector.tensor_copy(v2s[:], tab2s_raw[:].indirect(l2[:]))
-        v2w = []
+        v2w = held("v2w", [P, 2, S], U32, tag="wd_raw1")
         for a in range(2):
-            tile = held("v2w%d" % a, [P, S], U32)
-            nc.vector.tensor_copy(tile[:], tab2w[a][:].bitcast(U32).indirect(l2[:]))
-            v2w.append(tile)
-        h1_scatter(6)
+            nc.vector.tensor_copy(v2w[:, a, :], tab2w[a][:].bitcast(U32).indirect(l2[:]))
+        for s in range(4, 7):
+            h1_scatter(s)
         w3_q = {}
         for a in range(2):
-            wide = cast_dealt("w3_wide%d0" % a, w3_raw[a, 0])
+            wide = cast_dealt("w3_wide%d0" % a, w3_raw[a, 0], "cast%d" % a)
             w3_q[a, 0] = quantise("w3_%d0" % a, "w3_%d" % a, wide[:], HALF)
         h1_scatter(7)
 
@@ -235,9 +255,12 @@ def tile_list_pasta_crack_page_kernel(
             acc = bank("h2_%d" % s, t)
             for a in range(2):
                 nc.tensor.matmul_mx(out=acc[:], lhsT=w3_q[a, b][0][:, cols].bitcast(FP8X4),
-                                    lhsT_scale=w3_q[a, b][1][:, cols], rhs=v2w[a][:].bitcast(FP8X4),
+                                    lhsT_scale=w3_q[a, b][1][:, cols], rhs=v2w[:, a, :].bitcast(FP8X4),
                                     rhs_scale=v2s[4 * a : P, :], start=(a == 0), stop=(a == 1))
-            h2[s] = ring.tile([P, S], F32, name="h2_sb%d" % s, tag="th")
+            if s < 2:
+                h2[s] = held("h2_sb%d" % s, [P, S], F32, tag="cast%d" % s)
+            else:
+                h2[s] = ring.tile([P, S], F32, name="h2_sb%d" % s, tag="th")
             nc.vector.tensor_tensor(h2[s][:], acc[:], air_t[b][:, t, :], ALU.max)
 
         def h2_scatter(s):
@@ -268,15 +291,16 @@ def tile_list_pasta_crack_page_kernel(
                 h2_max(s + 1)
             if s == 2:
                 for a in range(2):
-                    wide = cast_dealt("w3_wide%d1" % a, w3_raw[a, 1])
+                    wide = cast_dealt("w3_wide%d1" % a, w3_raw[a, 1], "cast%d" % a)
                     w3_q[a, 1] = quantise("w3_%d1" % a, "w3_%d" % a, wide[:], HALF)
             if s < 7:
                 h2_scatter(s)
             pick(s - 1)
             if s == 4:
-                w5w = held("w5w", [P, 2, 4, P], I32)
-                nc.vector.tensor_copy(w5w[:], w5w_raw[:].rearrange("p a (m t) -> p a t m", t=4))
-                w5s = held("w5s", [P, 4, P], U8)
+                w5w = held("w5w", [P, 2, 4, P], I32, tag="air0")
+                nc.vector.tensor_copy(w5w[:].rearrange("p a t (g i) -> p a g t i", i=4),
+                                      w5w_raw[:].rearrange("p a (g i t) -> p a g t i", i=4, t=4))
+                w5s = held("w5s", [P, 4, P], U8, tag="cast0")
                 nc.vector.tensor_copy(w5s[:], w5s_raw[:].rearrange("p (m t) -> p t m", t=4))
             if s == 5:
                 x0_q = quantise("x0", "x0", x0_wide[:].rearrange("p c t -> p (c t)"), PICK, codes_tag="tabs_raw")

from contextlib import ExitStack

import concourse.mybir as mybir
from concourse.masks import make_identity

F32 = mybir.dt.float32
BF16 = mybir.dt.bfloat16
I32 = mybir.dt.int32
U32 = mybir.dt.uint32
U16 = mybir.dt.uint16
U8 = mybir.dt.uint8
FP8X4 = mybir.dt.float8_e4m3fn_x4
FP4X4 = mybir.dt.float4_e2m1fn_x4
ALU = mybir.AluOpType
ACT = mybir.ActivationFunctionType

P = 128
K, K3, H, N, T, T2, S, PICK = 1024, 512, 1024, 512, 2048, 2048, 512, 1024
FLOPS = 2 * (K * H * S + K3 * H * S + K * H * S + H * N * PICK)
HALF = 512
CH = 256


def tile_list_pasta_crack_page_kernel(
    tc, tab_words, tab_scales, offs, tab2_words, tab2_scales, offs2, offs3, offs4, offs5,
    w1_words, w1_scales, wd, dies, g1, w3, air, wg1, wg2, page0, gain, w5_words, w5_scales, season,
    out_0, out_1, out_2,
):
    nc = tc.nc
    with ExitStack() as ctx:
        lists = ctx.enter_context(tc.tile_pool(name="lists", bufs=1))
        keep = ctx.enter_context(tc.tile_pool(name="keep", bufs=1))
        ring = ctx.enter_context(tc.tile_pool(name="ring", bufs=3))
        psum = ctx.enter_context(tc.psum_pool(name="psum", bufs=1))

        def held(name, shape, dtype, tag=None):
            return keep.tile(shape, dtype, name=name, tag=tag or name, align_bytes=64)

        def load(dst, src):
            nc.sync.dma_start(out=dst, in_=src)

        def load_list(name, src):
            tile = lists.tile(list(src.shape), U16, name=name)
            nc.sync.dma_start(tile[:], src)
            return tile

        def load_rows4(name, slot, src):
            tile = held(name, [P, 4, src.shape[1]], F32, tag=slot)
            load(tile[:], src.rearrange("(p j) c -> p j c", j=4))
            return tile

        def load_words(name, slot, words, a):
            tile = held(name, [P, T], I32, tag=slot)
            load(tile[:], words[a].rearrange("p c i -> p (c i)").bitcast(I32))
            return tile

        def load_scales_side(queue, tile, scales):
            for q in range(4):
                queue.dma_start(out=tile[32 * q : 32 * q + 4, :, :].bitcast(I32),
                                in_=scales.bitcast(I32)[:, 4 * q : 4 * q + 4, :].rearrange("a r c -> r a c"))

        def load_scales_stacked(tile, scales):
            for q in range(4):
                load(tile[32 * q : 32 * q + 8, :].bitcast(I32), scales.bitcast(I32)[:, 4 * q : 4 * q + 4, :])

        def load_page(s):
            b, t = divmod(s, 4)
            tile = held("page%d" % s, [P, T2], F32)
            load(tile[:], page0[HALF * b : HALF * (b + 1), :].rearrange("(p t) c -> p t c", t=4)[:, t, :])
            return tile

        tabs_raw = held("tabs_raw", [P, 2, T], U8)
        w1s_raw = held("w1s_raw", [P, 2, H], U8)
        tab2s_raw = held("tab2s_raw", [P, T], U8)
        w5s_raw = held("w5s_raw", [P, N], U8)
        nc.vector.memset(w1s_raw[:].bitcast(I32), 0)
        nc.vector.memset(tabs_raw[:].bitcast(I32), 0)
        ident = held("ident", [P, P], F32)
        make_identity(nc, ident[:])
        nc.vector.memset(tab2s_raw[:].bitcast(I32), 0)
        nc.vector.memset(w5s_raw[:].bitcast(I32), 0)
        warm = held("warm", [P, 8], F32)
        warm2 = held("warm2", [P, 8], F32)
        nc.vector.memset(warm[:], 0.0)
        nc.scalar.activation(warm2[:], warm[:], ACT.Tanh)

        wg1_raw = held("wg1_raw", [P, S], F32)
        load(wg1_raw[:], wg1)
        w1w_raw = held("w1w_raw", [P, 2, H // 2], I32, tag="wraw")
        load(w1w_raw[:], w1_words.bitcast(I32).rearrange("a p c -> p a c"))
        l1 = load_list("l1", offs)
        g1_t = held("g1_t", [P, 2, 4], F32)
        load(g1_t[:], g1.rearrange("(b p t) -> p b t", b=2, t=4))
        l3 = load_list("l3", offs3)
        dies_raw = load_rows4("dies_raw", "dies_raw", dies)
        wd_raw = [load_rows4("wd_raw0", "wd_raw0", wd[:, 0:HALF])]
        l2 = load_list("l2", offs2)
        load_scales_side(nc.sync, tabs_raw, tab_scales)
        tabw = [load_words("tabw0", "tabw0", tab_words, 0)]
        load_scales_side(nc.sync, w1s_raw, w1_scales)
        tabw.append(load_words("tabw1", "tabw1", tab_words, 1))
        pages = [load_page(s) for s in range(2)]
        wg2_raw = held("wg2_raw", [P, S], F32)
        load(wg2_raw[:], wg2)
        wd_raw.append(load_rows4("wd_raw1", "wd_raw1", wd[:, HALF:H]))
        load_scales_stacked(tab2s_raw, tab2_scales)
        pages.append(load_page(2))
        pages.append(load_page(3))

        def cast_dealt(name, raw, tag):
            wide = held(name, [P, 4 * HALF], BF16, tag=tag)
            nc.scalar.copy(wide[:].rearrange("p (t m j) -> p m j t", t=4, j=4),
                           raw[:].rearrange("p j (m t) -> p m j t", t=4))
            return wide

        def cast_plain(eng, dst, src):
            out = dst.rearrange("p (c i j) -> p c j i", i=4, j=4)
            in_ = src.rearrange("p j (c i) -> p c j i", i=4)
            if eng == "scalar":
                nc.scalar.copy(out, in_)
            else:
                nc.vector.tensor_copy(out, in_)

        def quantise(name, tag, wide, cols, codes_tag=None):
            codes = held(name + "_c", [P, cols], U32, tag=codes_tag or tag + "_c")
            plane = held(name + "_s", [P, cols], U8, tag=tag + "_s")
            nc.vector.quantize_mx(out=codes[:].bitcast(FP8X4), scales=plane[:], in_=wide)
            return codes, plane

        def bank(name, n):
            return psum.tile([P, HALF], F32, name=name, tag="bank%d" % n)

        def spread_rows(name, raw, first_bank):
            turned = bank(name + "_turned", first_bank)
            for u in range(4):
                nc.tensor.transpose(turned[:, P * u : P * (u + 1)], raw[:, P * u : P * (u + 1)], ident[:])
            picked_cols = held(name + "_cols", [P, 4, 4, 4, 32], F32, tag="air0")
            nc.scalar.copy(picked_cols[:],
                           turned[:].rearrange("p (u m t) -> p u t m", u=4, t=4).unsqueeze(3).broadcast_to([P, 4, 4, 4, 32]))
            return picked_cols

        def spread_back(name, picked_cols):
            rows = held(name + "_rows", [P, 4, S], F32)
            for t in range(4):
                back = bank(name + "_back%d" % t, t)
                for u in range(4):
                    nc.tensor.transpose(back[:, P * u : P * (u + 1)],
                                        picked_cols[:, u, t, :, :].rearrange("p q m -> p (q m)"), ident[:])
                nc.scalar.copy(rows[:, t, :], back[:])
            return rows

        wg1_cols = spread_rows("wg1", wg1_raw, 0)

        w1w, w1s = [], []
        for b in range(2):
            ww = held("w1w%d" % b, [P, 2, 4, 2 * P], U8)
            nc.vector.tensor_copy(
                ww[:].rearrange("p a t (m e) -> p a t m e", e=2),
                w1w_raw[:].bitcast(U8)[:, :, H * b : H * (b + 1)].rearrange("p a (m t e) -> p a t m e", t=4, e=2))
            w1w.append(ww)

        def deal_w1_scales(b, tag):
            ws = held("w1s%d" % b, [P, 2, 4, P], U8, tag=tag)
            nc.vector.tensor_copy(
                ws[:], w1s_raw[:, :, HALF * b : HALF * (b + 1)].rearrange("p a (m t) -> p a t m", t=4))
            w1s.append(ws)

        dies_wide = held("dies_wide", [P, 4 * S], BF16, tag="cast0")
        cast_plain("vector", dies_wide[:], dies_raw[:])
        wd_wide = cast_dealt("wd_wide0", wd_raw[0], "cast1")
        wg1_t = spread_back("wg1", wg1_cols)
        dies_q = quantise("dies", "dies", dies_wide[:], S)
        vs = []
        for a in range(2):
            tile = held("vs%d" % a, [P, S], U8)
            nc.vector.tensor_copy(tile[:], tabs_raw[:, a, :].indirect(l1[:]))
            vs.append(tile)
        wd_q = [quantise("wd0", "wd0", wd_wide[:], HALF, codes_tag="tabs_raw")]
        vw = []
        for a in range(2):
            tile = held("vw%d" % a, [P, S], U32)
            nc.vector.tensor_copy(tile[:], tabw[a][:].bitcast(U32).indirect(l1[:]))
            vw.append(tile)
            deal_w1_scales(a, ("w1s0", "tabw1")[a])

        def h1_scatter(s):
            b, t = divmod(s, 4)
            cols = slice(P * t, P * (t + 1))
            acc = bank("h1_%d" % s, 4 + t)
            nc.tensor.matmul_mx(out=acc[:], lhsT=wd_q[b][0][:, cols].bitcast(FP8X4), lhsT_scale=wd_q[b][1][:, cols],
                                rhs=dies_q[0][:].bitcast(FP8X4), rhs_scale=dies_q[1][:], start=True, stop=False)
            for a in range(2):
                nc.tensor.matmul_mx(out=acc[:], lhsT=w1w[b][:, a, t, :].bitcast(FP4X4), lhsT_scale=w1s[b][:, a, t, :],
                                    rhs=vw[a][:].bitcast(FP8X4), rhs_scale=vs[a][:], start=False, stop=(a == 1))
            if s in (0, 2, 4, 5):
                th = held("th%d" % s, [P, S], F32, tag="v2s" if s == 2 else "cast%d" % (s % 2))
            else:
                th = ring.tile([P, S], F32, name="th%d" % s, tag="th")
            nc.scalar.activation(th[:], acc[:], ACT.Tanh)
            h1 = held("h1_sb%d" % s, [P, S], F32, tag=("wd_raw1", "w3_raw10")[b]) if t == 3 else th
            nc.scalar.activation(h1[:], th[:], ACT.Copy, scale=g1_t[:, b, t : t + 1])
            nc.vector.tensor_tensor(pages[s][:].indirect(l3[:]), h1[:], wg1_t[:, t, :], ALU.mult)

        for s in range(4):
            if s == 3:
                wd_q.append(quantise("wd1", "wd1", cast_dealt("wd_wide1", wd_raw[1], "cast0")[:], HALF))
            h1_scatter(s)

        wg2_t = spread_back("wg2", spread_rows("wg2", wg2_raw, 4))
        tab2w = [load_words("tab2w0", "tab2w0", tab2_words, 0), load_words("tab2w1", "dies_raw", tab2_words, 1)]
        pages.append(load_page(4))
        pages.append(load_page(5))
        pages.append(load_page(6))
        w3_raw = {}
        w3_raw[0, 0] = load_rows4("w3_raw00", "w3_raw00", w3[0:HALF, 0:HALF])
        w3_raw[1, 0] = load_rows4("w3_raw10", "w3_raw10", w3[HALF:K, 0:HALF])
        pages.append(load_page(7))
        l4 = load_list("l4", offs4)
        air_t = [load_rows4("air0", "air0", air[0:HALF, :])]
        l5 = load_list("l5", offs5)
        gain_t = held("gain_t", [P, 2, 4], F32)
        load(gain_t[:], gain.rearrange("(b p t) -> p b t", b=2, t=4))

        v2s = held("v2s", [P, S], U8)
        nc.vector.tensor_copy(v2s[:], tab2s_raw[:].indirect(l2[:]))
        v2w = held("v2w", [P, 2, S], U32, tag="wd_raw1")
        for a in range(2):
            nc.vector.tensor_copy(v2w[:, a, :], tab2w[a][:].bitcast(U32).indirect(l2[:]))
        for s in range(4, 7):
            h1_scatter(s)
        w3_q = {}
        for a in range(2):
            wide = cast_dealt("w3_wide%d0" % a, w3_raw[a, 0], "cast%d" % a)
            w3_q[a, 0] = quantise("w3_%d0" % a, "w3_%d" % a, wide[:], HALF)
        h1_scatter(7)

        w3_raw[0, 1] = load_rows4("w3_raw01", "wd_raw0", w3[0:HALF, HALF:H])
        w3_raw[1, 1] = load_rows4("w3_raw11", "tabw0", w3[HALF:K, HALF:H])
        air_t.append(load_rows4("air1", "tabw1", air[HALF:H, :]))
        w5w_raw = held("w5w_raw", [P, 2, N], I32, tag="wraw")
        load(w5w_raw[:], w5_words.rearrange("a p c i -> p a (c i)").bitcast(I32))
        load_scales_stacked(w5s_raw, w5_scales)
        season_rows = season.rearrange("(p t) j -> p t j", t=4)
        y = []
        for h in range(2):
            tile = held("y%d" % h, [P, 4, HALF], F32, tag=("wd_raw1", "tab2w0")[h])
            load(tile[:], season_rows[:, :, HALF * h : HALF * (h + 1)])
            y.append(tile)

        h2 = {}

        def h2_max(s):
            b, t = divmod(s, 4)
            cols = slice(P * t, P * (t + 1))
            acc = bank("h2_%d" % s, t)
            for a in range(2):
                nc.tensor.matmul_mx(out=acc[:], lhsT=w3_q[a, b][0][:, cols].bitcast(FP8X4),
                                    lhsT_scale=w3_q[a, b][1][:, cols], rhs=v2w[:, a, :].bitcast(FP8X4),
                                    rhs_scale=v2s[4 * a : P, :], start=(a == 0), stop=(a == 1))
            if s < 2:
                h2[s] = held("h2_sb%d" % s, [P, S], F32, tag="cast%d" % s)
            else:
                h2[s] = ring.tile([P, S], F32, name="h2_sb%d" % s, tag="th")
            nc.vector.tensor_tensor(h2[s][:], acc[:], air_t[b][:, t, :], ALU.max)

        def h2_scatter(s):
            nc.vector.tensor_tensor(pages[s][:].indirect(l4[:]), h2[s][:], wg2_t[:, s % 4, :], ALU.mult)

        small_tags = ("vw0", "vw1", "w1w0", "w1w1")
        x0_wide = held("x0_wide", [P, PICK, 4], BF16, tag="w3_raw00")
        x1_wide = [held("x1_wide%d" % c, [P, CH, 4], BF16, tag=small_tags[c]) for c in range(PICK // CH)]

        def gained(s, dst, src):
            b, t = divmod(s, 4)
            nc.scalar.activation(dst[:, :, t], src, ACT.Copy, scale=gain_t[:, b, t : t + 1])

        def pick(s):
            picked = ring.tile([P, PICK], F32, name="picked%d" % s, tag="picked", bufs=2)
            nc.vector.tensor_copy(picked[:], pages[s][:].indirect(l5[:]))
            if s < 4:
                gained(s, x0_wide, picked[:])
            else:
                for c in range(PICK // CH):
                    gained(s, x1_wide[c], picked[:, CH * c : CH * (c + 1)])

        h2_max(0)
        h2_max(1)
        h2_scatter(0)
        for s in range(1, 8):
            if s < 7:
                h2_max(s + 1)
            if s == 2:
                for a in range(2):
                    wide = cast_dealt("w3_wide%d1" % a, w3_raw[a, 1], "cast%d" % a)
                    w3_q[a, 1] = quantise("w3_%d1" % a, "w3_%d" % a, wide[:], HALF)
            if s < 7:
                h2_scatter(s)
            pick(s - 1)
            if s == 4:
                w5w = held("w5w", [P, 2, 4, P], I32, tag="air0")
                nc.vector.tensor_copy(w5w[:].rearrange("p a t (g i) -> p a g t i", i=4),
                                      w5w_raw[:].rearrange("p a (g i t) -> p a g t i", i=4, t=4))
                w5s = held("w5s", [P, 4, P], U8, tag="cast0")
                nc.vector.tensor_copy(w5s[:], w5s_raw[:].rearrange("p (m t) -> p t m", t=4))
            if s == 5:
                x0_q = quantise("x0", "x0", x0_wide[:].rearrange("p c t -> p (c t)"), PICK, codes_tag="tabs_raw")
        h2_scatter(7)

        def y_pass(acc, a, t, codes, plane, start, stop):
            nc.tensor.matmul_mx(out=acc, lhsT=w5w[:, a, t, :].bitcast(FP8X4), lhsT_scale=w5s[4 * a : P, t, :],
                                rhs=codes.bitcast(FP8X4), rhs_scale=plane, start=start, stop=stop)

        y_acc = {}
        for h in range(2):
            for t in range(4):
                y_acc[h, t] = bank("y_%d%d" % (h, t), 4 * (1 - h) + t)
                cols = slice(HALF * h, HALF * (h + 1))
                y_pass(y_acc[h, t][:], 0, t, x0_q[0][:, cols], x0_q[1][:, cols], True, False)

        last = ring.tile([P, PICK], F32, name="picked7", tag="picked", bufs=2)
        for c in range(PICK // CH):
            part = last[:, CH * c : CH * (c + 1)]
            nc.vector.tensor_copy(part, pages[7][:].indirect(l5[:, CH // 16 * c : CH // 16 * (c + 1)]))
            gained(7, x1_wide[c], part)

        for c in range(PICK // CH):
            h, u = divmod(c, 2)
            codes, plane = quantise("x1_%d" % c, "x1_%d" % c, x1_wide[c][:].rearrange("p c t -> p (c t)"), CH)
            for t in range(4):
                y_pass(y_acc[h, t][:, CH * u : CH * (u + 1)], 1, t, codes[:], plane[:], False, u == 1)

        out_rows = out_0.rearrange("(p t) j -> p t j", t=4)
        out_words = out_1[0].rearrange("p m t -> p (m t)").bitcast(I32)
        out_scales = out_2[0].bitcast(I32)
        y_plane = held("y_plane", [P, PICK], U8)
        y_codes = [held("y_codes%d" % c, [P, CH], I32) for c in range(PICK // CH)]
        for h in range(2):
            for t in range(4):
                nc.vector.tensor_tensor(y[h][:, t, :], y_acc[h, t][:], y[h][:, t, :], ALU.add)
                nc.sync.dma_start(out=out_rows[:, t, HALF * h : HALF * (h + 1)], in_=y[h][:, t, :])
        for c in range(PICK // CH):
            h, u = divmod(c, 2)
            y_wide = held("y_wide%d" % c, [P, 4 * CH], BF16, tag=small_tags[c])
            cast_plain("vector" if c == 3 else "scalar", y_wide[:], y[h][:, :, CH * u : CH * (u + 1)])
            nc.vector.quantize_mx(out=y_codes[c][:].bitcast(FP8X4), scales=y_plane[:, CH * c : CH * (c + 1)],
                                  in_=y_wide[:])
            nc.sync.dma_start(out=out_words[:, CH * c : CH * (c + 1)], in_=y_codes[c][:])
        for q in range(4):
            nc.sync.dma_start(out=out_scales[4 * q : 4 * q + 4, :], in_=y_plane[32 * q : 32 * q + 4, :].bitcast(I32))
